import numpy as np
import ml_dtypes


def mxq(x, axis, fmt="e4m3"):
    dtype, down = {"e4m3": (ml_dtypes.float8_e4m3fn, 7), "e5m2": (ml_dtypes.float8_e5m2, 14)}[fmt]
    v = np.moveaxis(np.asarray(x, np.float32).astype(ml_dtypes.bfloat16).astype(np.float64), axis, -1)
    blocks = v.reshape(v.shape[:-1] + (-1, 32))
    amax = np.abs(blocks).max(-1, keepdims=True)
    byte = np.maximum(np.where(amax > 0, np.frexp(amax)[1] - 1 + 127, 0) - down, 1)
    scale = np.exp2(byte - 127.0)
    codes = (blocks / scale).astype(np.float32).astype(dtype).astype(np.float64)
    return np.moveaxis((codes * scale).reshape(v.shape), -1, axis)


WIDE = False


def mx_kscale(k):
    if not WIDE:
        return np.ones(k)
    levels = np.array([10, -10, 5, -5, 0])
    if k % 512:
        return np.exp2(np.random.permutation(np.resize(levels, k // 32))).repeat(32)
    a = np.empty((k // 512, 16))
    for p in range(k // 512):
        a[p, :8] = np.random.permutation(np.resize(levels, 8))
        for g in range(8):
            far = levels[np.abs(levels - a[p, g]) >= 10]
            a[p, g + 8] = far[np.random.randint(len(far))]
    return np.exp2(a.ravel()).repeat(32)


def f64(x):
    return np.asarray(x).astype(np.float64)


def striped(idx):
    return np.tile(idx.reshape(-1, 16).T, (8, 1)).astype(np.uint16)


def unstriped(offs):
    return offs[:16].T.reshape(-1).astype(np.int64)


def relu(v):
    return np.maximum(v, 0.0)


K, T, E, C, H, N = 1024, 1024, 8, 128, 512, 128


def by_expert(wq, xq):
    return np.concatenate([wq[e].T @ xq[:, e * C:(e + 1) * C] for e in range(E)], axis=1)


def setup_inputs():
    n = np.random.standard_normal
    s = mx_kscale(K)[:, None]
    u = mx_kscale(H)
    return {
        "xT": (n((K, T)) * s).astype(np.float32),
        "w1": (n((E, K, H)) / np.sqrt(K) / s[None] * u[None, None, :]).astype(np.float32),
        "w2": (n((E, H, N)) / np.sqrt(H) / u[None, :, None]).astype(np.float32),
        "gate": np.tile(np.random.uniform(0.2, 1.0, E * C), (K, 1)).astype(np.float32),
        "offs": striped(np.random.permutation(T)[:E * C]),
    }


def reference(xT, w1, w2, gate, offs):
    idx = unstriped(offs)
    xq = mxq(f64(gate) * f64(xT)[:, idx], 0, "e4m3")
    h = relu(by_expert(mxq(f64(w1), 1, "e4m3"), xq))
    y = by_expert(mxq(f64(w2), 1, "e4m3"), mxq(h, 0, "e4m3"))
    out = np.zeros((N, T))
    out[:, idx] = y
    return out

@@ -1,0 +1,229 @@
+from contextlib import ExitStack
+
+import concourse.mybir as mybir
+
+K, T, E, C, H, N = 1024, 1024, 8, 128, 512, 128
+FLOPS = 2 * E * C * (K * H + H * N)
+BYTES = 4 * (K * T + E * K * H + E * H * N + E * C + N * T) + 2 * 128 * (E * C // 16)
+
+F32 = mybir.dt.float32
+BF16 = mybir.dt.bfloat16
+U32 = mybir.dt.uint32
+U16 = mybir.dt.uint16
+U8 = mybir.dt.uint8
+FP8X4 = mybir.dt.float8_e4m3fn_x4
+MULT = mybir.AluOpType.mult
+RELU = mybir.ActivationFunctionType.Relu
+
+P = 128
+PACK = 4
+K_PASS = P * PACK
+PASSES = K // K_PASS
+HALVES = 2
+HALF = E * C // HALVES
+LIST_ROWS = 16
+LOADS = "gxgWxWxWxWxWxWxWxWWWwWwWWwWwWwWwww"
+VSET = [8,10,12,14]
+XV = [[1,1]]
+V2 = []
+LAST = E * PASSES - 1
+
+
+def tile_moe_pre_mlp_relu_kernel(tc, xT, w1, w2, gate, offs, out):
+    nc = tc.nc
+    with ExitStack() as ctx:
+        keep = ctx.enter_context(tc.tile_pool(name="keep", bufs=1))
+        w1_raw_pool = ctx.enter_context(tc.tile_pool(name="w1_raw", bufs=7))
+        w2_raw_pool = ctx.enter_context(tc.tile_pool(name="w2_raw", bufs=4))
+        w1_bf_pool = ctx.enter_context(tc.tile_pool(name="w1_bf", bufs=5))
+        w1_mx_pool = ctx.enter_context(tc.tile_pool(name="w1_mx", bufs=10))
+        gath_pool = ctx.enter_context(tc.tile_pool(name="gath", bufs=4))
+        small = ctx.enter_context(tc.tile_pool(name="small", bufs=2))
+        y_pool = ctx.enter_context(tc.tile_pool(name="y_pool", bufs=3))
+        psum = ctx.enter_context(tc.psum_pool(name="psum", bufs=2))
+
+        offsets = keep.tile([P, E * C // LIST_ROWS], U16, name="offsets")
+        nc.sync.dma_start(offsets[:], offs)
+        gate_rows = {}
+        x_rows = {}
+        w1_raw = {}
+        w2_raw = {}
+
+        def load_gate(h):
+            gate_rows[h] = keep.tile([P, HALF], F32, name="gate_row%d" % h)
+            nc.sync.dma_start(out=gate_rows[h][:], in_=gate[0:P, h * HALF : (h + 1) * HALF])
+
+        def load_x(s):
+            g, j = divmod(s, PACK)
+            x_rows[s] = keep.tile([P, T], F32, name="x_rows%d" % s)
+            rows = xT[g * K_PASS : (g + 1) * K_PASS, :].rearrange("(p j) t -> p j t", j=PACK)
+            nc.sync.dma_start(out=x_rows[s][:], in_=rows[:, j, :])
+
+        def load_w1(k):
+            e, g = divmod(k, PASSES)
+            rows = w1[e, g * K_PASS : (g + 1) * K_PASS, :].rearrange("(p j) c -> p j c", j=PACK)
+            if k == LAST:
+                w1_raw[k] = []
+                for a in range(2):
+                    part = keep.tile([P, PACK, H // 2], F32, name="w1_last%d" % a)
+                    nc.sync.dma_start(out=part[:], in_=rows[:, :, a * (H // 2) : (a + 1) * (H // 2)])
+                    w1_raw[k].append(part)
+                return
+            w1_raw[k] = w1_raw_pool.tile([P, PACK, H], F32, name="w1_raw")
+            nc.sync.dma_start(out=w1_raw[k][:], in_=rows)
+
+        def load_w2(e):
+            w2_raw[e] = w2_raw_pool.tile([P, PACK, N], F32, name="w2_raw")
+            nc.sync.dma_start(out=w2_raw[e][:], in_=w2[e].rearrange("(p j) n -> p j n", j=PACK))
+
+        steps = []
+        seen = {"x": 0, "W": 0, "w": 0, "g": 0}
+        for ch in LOADS:
+            steps.append((ch, seen[ch]))
+            seen[ch] = seen[ch] + 1
+        loaders = {"x": load_x, "W": load_w1, "w": load_w2, "g": load_gate}
+        for ch, k in steps:
+            loaders[ch](k)
+
+        def copy_on(on_vector, dst, src):
+            if on_vector:
+                nc.vector.tensor_copy(out=dst, in_=src)
+            else:
+                nc.scalar.copy(out=dst, in_=src)
+
+        def interleave(on_vector, dst, src):
+            copy_on(
+                on_vector,
+                dst.rearrange("p (c i j) -> p c j i", i=PACK, j=PACK),
+                src.rearrange("p j (c i) -> p c j i", i=PACK),
+            )
+
+        def quantize(pool, name, grouped, width):
+            codes = pool.tile([P, width], U32, name=name + "_codes", align_bytes=64)
+            scales = pool.tile([P, width], U8, name=name + "_scales", align_bytes=64)
+            nc.vector.quantize_mx(out=codes[:].bitcast(FP8X4), scales=scales[:], in_=grouped)
+            return codes, scales
+
+        gathered = {}
+        x_mx = {}
+        w1_mx = {}
+        w2_mx = {}
+        h_bf = {}
+
+        def gather(s, h):
+            g, j = divmod(s, PACK)
+            if j == 0:
+                gathered[g, h] = gath_pool.tile([P, PACK, HALF], F32, name="gathered")
+            cols = HALF // LIST_ROWS
+            nc.vector.tensor_tensor(
+                out=gathered[g, h][:, j, :],
+                in0=x_rows[s][:].indirect(offsets[:, h * cols : (h + 1) * cols]),
+                in1=gate_rows[h][:],
+                op=MULT,
+            )
+
+        def make_x(g, h):
+            x_bf = small.tile([P, HALF * PACK], BF16, name="x_bf", align_bytes=64)
+            interleave([g, h] in XV, x_bf[:], gathered[g, h][:])
+            x_mx[g, h] = quantize(keep, "x%d%d" % (g, h), x_bf[:], HALF)
+
+        def make_w1(k):
+            if k == LAST:
+                halves = [keep.tile([P, H * PACK // 2], BF16, name="w1_last_bf%d" % u, align_bytes=64) for u in range(2)]
+                for a in range(2):
+                    src = w1_raw[k][a][:].rearrange("p j (m t) -> p m j t", t=PACK)
+                    for u in range(2):
+                        dst = halves[u][:].rearrange("p (t m j) -> p m j t", t=2, j=PACK)
+                        copy_on(u == 0, dst[:, a * (P // 2) : (a + 1) * (P // 2), :, :], src[:, :, :, 2 * u : 2 * u + 2])
+                pairs = [quantize(keep, "w1_last%d" % u, halves[u][:], H // 2) for u in range(2)]
+                w1_mx[k] = [
+                    (pairs[t // 2][0][:, (t % 2) * P : (t % 2 + 1) * P], pairs[t // 2][1][:, (t % 2) * P : (t % 2 + 1) * P])
+                    for t in range(PACK)
+                ]
+                return
+            w1_bf = w1_bf_pool.tile([P, H * PACK], BF16, name="w1_bf", align_bytes=64)
+            copy_on(
+                k in VSET,
+                w1_bf[:].rearrange("p (t m j) -> p m j t", t=PACK, j=PACK),
+                w1_raw[k][:].rearrange("p j (m t) -> p m j t", t=PACK),
+            )
+            codes, scales = quantize(w1_mx_pool, "w1", w1_bf[:], H)
+            w1_mx[k] = [(codes[:, t * P : (t + 1) * P], scales[:, t * P : (t + 1) * P]) for t in range(PACK)]
+
+        def make_w2(e):
+            w2_bf = small.tile([P, N * PACK], BF16, name="w2_bf", align_bytes=64)
+            interleave(e in V2, w2_bf[:], w2_raw[e][:])
+            w2_mx[e] = quantize(keep, "w2_%d" % e, w2_bf[:], N)
+
+        def first_layer(e):
+            h, place = divmod(e * C, HALF)
+            slots = slice(place, place + C)
+            acc = psum.tile([P, PACK, C], F32, name="acc_h")
+            for t in range(PACK):
+                for g in range(PASSES):
+                    w_codes, w_scales = w1_mx[e * PASSES + g][t]
+                    x_codes, x_scales = x_mx[g, h]
+                    nc.tensor.matmul_mx(
+                        out=acc[:, t, :],
+                        lhsT=w_codes.bitcast(FP8X4),
+                        lhsT_scale=w_scales,
+                        rhs=x_codes[:, slots].bitcast(FP8X4),
+                        rhs_scale=x_scales[:, slots],
+                        start=(g == 0),
+                        stop=(g == PASSES - 1),
+                    )
+            h_bf[e] = small.tile([P, C * PACK], BF16, name="h_bf", align_bytes=64)
+            nc.scalar.activation(
+                out=h_bf[e][:].rearrange("p (s t) -> p s t", t=PACK),
+                in_=acc[:].rearrange("p t s -> p s t"),
+                func=RELU,
+            )
+
+        result = keep.tile([P, T], F32, name="result")
+
+        def second_layer(e):
+            h_codes, h_scales = quantize(small, "h", h_bf[e][:], C)
+            w_codes, w_scales = w2_mx[e]
+            acc = psum.tile([P, C], F32, name="acc_y")
+            nc.tensor.matmul_mx(
+                out=acc[:],
+                lhsT=w_codes[:].bitcast(FP8X4),
+                lhsT_scale=w_scales[:],
+                rhs=h_codes[:].bitcast(FP8X4),
+                rhs_scale=h_scales[:],
+                start=True,
+                stop=True,
+            )
+            y_sb = y_pool.tile([P, C], F32, name="y_sb")
+            nc.scalar.copy(out=y_sb[:], in_=acc[:])
+            cols = C // LIST_ROWS
+            nc.vector.tensor_copy(
+                out=result[:].indirect(offsets[:, e * cols : (e + 1) * cols]),
+                in_=y_sb[:],
+            )
+
+        done = set()
+
+        def follow_ups():
+            for g in range(PASSES):
+                for h in range(HALVES):
+                    if (g, h) not in x_mx and ("x", PACK * g + PACK - 1) in done:
+                        make_x(g, h)
+            for e in range(E):
+                if e not in h_bf and (2 * e + 1) in w1_mx and len(x_mx) == PASSES * HALVES:
+                    first_layer(e)
+                if ("y", e) not in done and e in h_bf and e in w2_mx:
+                    second_layer(e)
+                    done.add(("y", e))
+
+        for ch, k in steps:
+            if ch == "x":
+                for h in range(HALVES):
+                    gather(k, h)
+                done.add(("x", k))
+            elif ch == "W":
+                make_w1(k)
+            elif ch == "w":
+                make_w2(k)
+            follow_ups()
+        nc.sync.dma_start(out=out, in_=result[:])

@@ -1,6 +1,7 @@
 from contextlib import ExitStack
 
 import concourse.mybir as mybir
+from concourse.masks import make_identity
 
 K, T, E, C, H, N = 1024, 1024, 8, 128, 512, 128
 FLOPS = 2 * E * C * (K * H + H * N)
@@ -22,10 +23,12 @@ PASSES = K // K_PASS
 HALVES = 2
 HALF = E * C // HALVES
 LIST_ROWS = 16
-LOADS = "gxgWxWxWxWxWxWxWxWWWwWwWWwWwWwWwww"
-VSET = [8,10,12,14]
-XV = [[1,1]]
-V2 = []
+LOADS = "xWxWxWxxWxWxWxWWwWWwWWwWWwWWwwww"
+VSET = [9,11,13]
+XV = [[1,0],[1,1]]
+V2 = [7]
+HOLD = 10
+SLOTS = 10
 LAST = E * PASSES - 1
 
 
@@ -33,14 +36,15 @@ def tile_moe_pre_mlp_relu_kernel(tc, xT, w1, w2, gate, offs, out):
     nc = tc.nc
     with ExitStack() as ctx:
         keep = ctx.enter_context(tc.tile_pool(name="keep", bufs=1))
-        w1_raw_pool = ctx.enter_context(tc.tile_pool(name="w1_raw", bufs=7))
-        w2_raw_pool = ctx.enter_context(tc.tile_pool(name="w2_raw", bufs=4))
-        w1_bf_pool = ctx.enter_context(tc.tile_pool(name="w1_bf", bufs=5))
+        big_pool = ctx.enter_context(tc.tile_pool(name="big", bufs=1))
+        w1_bf_pool = ctx.enter_context(tc.tile_pool(name="w1_bf", bufs=6))
         w1_mx_pool = ctx.enter_context(tc.tile_pool(name="w1_mx", bufs=10))
         gath_pool = ctx.enter_context(tc.tile_pool(name="gath", bufs=4))
+        h_pool = ctx.enter_context(tc.tile_pool(name="h_pool", bufs=2))
         small = ctx.enter_context(tc.tile_pool(name="small", bufs=2))
         y_pool = ctx.enter_context(tc.tile_pool(name="y_pool", bufs=3))
         psum = ctx.enter_context(tc.psum_pool(name="psum", bufs=2))
+        psum_h = ctx.enter_context(tc.psum_pool(name="psum_h", bufs=6))
 
         offsets = keep.tile([P, E * C // LIST_ROWS], U16, name="offsets")
         nc.sync.dma_start(offsets[:], offs)
@@ -49,9 +53,26 @@ def tile_moe_pre_mlp_relu_kernel(tc, xT, w1, w2, gate, offs, out):
         w1_raw = {}
         w2_raw = {}
 
+        gate_cols = keep.tile([P, HALVES, PACK], F32, name="gate_cols")
+        nc.sync.dma_start(
+            out=gate_cols[:],
+            in_=gate[0, :].rearrange("(h p q) -> p h q", h=HALVES, q=PACK),
+        )
+
         def load_gate(h):
             gate_rows[h] = keep.tile([P, HALF], F32, name="gate_row%d" % h)
             nc.sync.dma_start(out=gate_rows[h][:], in_=gate[0:P, h * HALF : (h + 1) * HALF])
+
+        free_slots = list(range(SLOTS))
+        held = []
+
+        def slot_tile(shape, keep_slot=False):
+            slot = free_slots.pop(0)
+            if keep_slot:
+                held.append(slot)
+            else:
+                free_slots.append(slot)
+            return big_pool.tile(shape, F32, name="slot%d" % slot, align_bytes=64)
 
         def load_x(s):
             g, j = divmod(s, PACK)
@@ -65,15 +86,15 @@ def tile_moe_pre_mlp_relu_kernel(tc, xT, w1, w2, gate, offs, out):
             if k == LAST:
                 w1_raw[k] = []
                 for a in range(2):
-                    part = keep.tile([P, PACK, H // 2], F32, name="w1_last%d" % a)
+                    part = slot_tile([P, PACK, H // 2])
                     nc.sync.dma_start(out=part[:], in_=rows[:, :, a * (H // 2) : (a + 1) * (H // 2)])
                     w1_raw[k].append(part)
                 return
-            w1_raw[k] = w1_raw_pool.tile([P, PACK, H], F32, name="w1_raw")
+            w1_raw[k] = slot_tile([P, PACK, H], k == HOLD)
             nc.sync.dma_start(out=w1_raw[k][:], in_=rows)
 
         def load_w2(e):
-            w2_raw[e] = w2_raw_pool.tile([P, PACK, N], F32, name="w2_raw")
+            w2_raw[e] = slot_tile([P, PACK, N])
             nc.sync.dma_start(out=w2_raw[e][:], in_=w2[e].rearrange("(p j) n -> p j n", j=PACK))
 
         steps = []
@@ -84,6 +105,21 @@ def tile_moe_pre_mlp_relu_kernel(tc, xT, w1, w2, gate, offs, out):
         loaders = {"x": load_x, "W": load_w1, "w": load_w2, "g": load_gate}
         for ch, k in steps:
             loaders[ch](k)
+
+        ident = keep.tile([P, P], F32, name="ident")
+        make_identity(nc, ident[:])
+        for h in range(HALVES):
+            wide = small.tile([P, PACK, P], F32, name="wide")
+            nc.vector.tensor_copy(out=wide[:], in_=gate_cols[:, h, :].unsqueeze(2).to_broadcast([P, PACK, P]))
+            spread = psum.tile([P, PACK, P], F32, name="acc_y")
+            for q in range(PACK):
+                nc.tensor.transpose(spread[:, q, :], wide[:, q, :], ident[:])
+            gate_rows[h] = keep.tile([P, HALF], F32, name="gate_row%d" % h)
+            mover = nc.vector.tensor_copy if h == 0 else nc.scalar.copy
+            mover(
+                out=gate_rows[h][:].rearrange("p (n q) -> p n q", q=PACK),
+                in_=spread[:].rearrange("p q n -> p n q"),
+            )
 
         def copy_on(on_vector, dst, src):
             if on_vector:
@@ -109,6 +145,7 @@ def tile_moe_pre_mlp_relu_kernel(tc, xT, w1, w2, gate, offs, out):
         w1_mx = {}
         w2_mx = {}
         h_bf = {}
+        h_early = []
 
         def gather(s, h):
             g, j = divmod(s, PACK)
@@ -123,7 +160,7 @@ def tile_moe_pre_mlp_relu_kernel(tc, xT, w1, w2, gate, offs, out):
             )
 
         def make_x(g, h):
-            x_bf = small.tile([P, HALF * PACK], BF16, name="x_bf", align_bytes=64)
+            x_bf = w1_bf_pool.tile([P, HALF * PACK], BF16, name="w1_bf", align_bytes=64)
             interleave([g, h] in XV, x_bf[:], gathered[g, h][:])
             x_mx[g, h] = quantize(keep, "x%d%d" % (g, h), x_bf[:], HALF)
 
@@ -158,7 +195,7 @@ def tile_moe_pre_mlp_relu_kernel(tc, xT, w1, w2, gate, offs, out):
         def first_layer(e):
             h, place = divmod(e * C, HALF)
             slots = slice(place, place + C)
-            acc = psum.tile([P, PACK, C], F32, name="acc_h")
+            acc = psum_h.tile([P, PACK, C], F32, name="acc_h")
             for t in range(PACK):
                 for g in range(PASSES):
                     w_codes, w_scales = w1_mx[e * PASSES + g][t]
@@ -172,9 +209,17 @@ def tile_moe_pre_mlp_relu_kernel(tc, xT, w1, w2, gate, offs, out):
                         start=(g == 0),
                         stop=(g == PASSES - 1),
                     )
-            h_bf[e] = small.tile([P, C * PACK], BF16, name="h_bf", align_bytes=64)
+            if 2 * e < HOLD:
+                if e == 0:
+                    h_early.append(
+                        big_pool.tile([P, (HOLD + 1) // 2, C * PACK], BF16, name="slot%d" % held[0], align_bytes=64)
+                    )
+                h_bf[e] = h_early[0][:, e, :]
+            else:
+                h_late = h_pool.tile([P, C * PACK], BF16, name="h_bf", align_bytes=64)
+                h_bf[e] = h_late[:]
             nc.scalar.activation(
-                out=h_bf[e][:].rearrange("p (s t) -> p s t", t=PACK),
+                out=h_bf[e].rearrange("p (s t) -> p s t", t=PACK),
                 in_=acc[:].rearrange("p t s -> p s t"),
                 func=RELU,
             )
@@ -182,7 +227,7 @@ def tile_moe_pre_mlp_relu_kernel(tc, xT, w1, w2, gate, offs, out):
         result = keep.tile([P, T], F32, name="result")
 
         def second_layer(e):
-            h_codes, h_scales = quantize(small, "h", h_bf[e][:], C)
+            h_codes, h_scales = quantize(small, "h", h_bf[e], C)
             w_codes, w_scales = w2_mx[e]
             acc = psum.tile([P, C], F32, name="acc_y")
             nc.tensor.matmul_mx(
@@ -207,10 +252,10 @@ def tile_moe_pre_mlp_relu_kernel(tc, xT, w1, w2, gate, offs, out):
         def follow_ups():
             for g in range(PASSES):
                 for h in range(HALVES):
-                    if (g, h) not in x_mx and ("x", PACK * g + PACK - 1) in done:
+                    if (g, h) not in x_mx and ("x", PACK * g + PACK - 1, h) in done:
                         make_x(g, h)
             for e in range(E):
-                if e not in h_bf and (2 * e + 1) in w1_mx and len(x_mx) == PASSES * HALVES:
+                if e not in h_bf and (2 * e + 1) in w1_mx and (1, e * C // HALF) in x_mx and HOLD in w1_mx:
                     first_layer(e)
                 if ("y", e) not in done and e in h_bf and e in w2_mx:
                     second_layer(e)
@@ -220,7 +265,8 @@ def tile_moe_pre_mlp_relu_kernel(tc, xT, w1, w2, gate, offs, out):
             if ch == "x":
                 for h in range(HALVES):
                     gather(k, h)
-                done.add(("x", k))
+                    done.add(("x", k, h))
+                    follow_ups()
             elif ch == "W":
                 make_w1(k)
             elif ch == "w":

@@ -23,12 +23,12 @@ PASSES = K // K_PASS
 HALVES = 2
 HALF = E * C // HALVES
 LIST_ROWS = 16
-LOADS = "xWxWxWxxWxWxWxWWwWWwWWwWWwWWwwww"
-VSET = [9,11,13]
-XV = [[1,0],[1,1]]
+LOADS = "xxWxWxWxWxWxWxWWwWWwWWwWWwWWwwww"
+VSET = [11,13]
+XV = []
 V2 = [7]
 HOLD = 10
-SLOTS = 10
+SLOTS = 9
 LAST = E * PASSES - 1
 
 
@@ -37,9 +37,9 @@ def tile_moe_pre_mlp_relu_kernel(tc, xT, w1, w2, gate, offs, out):
     with ExitStack() as ctx:
         keep = ctx.enter_context(tc.tile_pool(name="keep", bufs=1))
         big_pool = ctx.enter_context(tc.tile_pool(name="big", bufs=1))
-        w1_bf_pool = ctx.enter_context(tc.tile_pool(name="w1_bf", bufs=6))
-        w1_mx_pool = ctx.enter_context(tc.tile_pool(name="w1_mx", bufs=10))
-        gath_pool = ctx.enter_context(tc.tile_pool(name="gath", bufs=4))
+        w1_bf_pool = ctx.enter_context(tc.tile_pool(name="w1_bf", bufs=10))
+        w1_mx_pool = ctx.enter_context(tc.tile_pool(name="w1_mx", bufs=8))
+        gath_pool = ctx.enter_context(tc.tile_pool(name="gath", bufs=3))
         h_pool = ctx.enter_context(tc.tile_pool(name="h_pool", bufs=2))
         small = ctx.enter_context(tc.tile_pool(name="small", bufs=2))
         y_pool = ctx.enter_context(tc.tile_pool(name="y_pool", bufs=3))
@@ -110,12 +110,12 @@ def tile_moe_pre_mlp_relu_kernel(tc, xT, w1, w2, gate, offs, out):
         make_identity(nc, ident[:])
         for h in range(HALVES):
             wide = small.tile([P, PACK, P], F32, name="wide")
-            nc.vector.tensor_copy(out=wide[:], in_=gate_cols[:, h, :].unsqueeze(2).to_broadcast([P, PACK, P]))
+            nc.scalar.copy(out=wide[:], in_=gate_cols[:, h, :].unsqueeze(2).to_broadcast([P, PACK, P]))
             spread = psum.tile([P, PACK, P], F32, name="acc_y")
             for q in range(PACK):
                 nc.tensor.transpose(spread[:, q, :], wide[:, q, :], ident[:])
             gate_rows[h] = keep.tile([P, HALF], F32, name="gate_row%d" % h)
-            mover = nc.vector.tensor_copy if h == 0 else nc.scalar.copy
+            mover = nc.scalar.copy
             mover(
                 out=gate_rows[h][:].rearrange("p (n q) -> p n q", q=PACK),
                 in_=spread[:].rearrange("p q n -> p n q"),
@@ -152,16 +152,19 @@ def tile_moe_pre_mlp_relu_kernel(tc, xT, w1, w2, gate, offs, out):
             if j == 0:
                 gathered[g, h] = gath_pool.tile([P, PACK, HALF], F32, name="gathered")
             cols = HALF // LIST_ROWS
-            nc.vector.tensor_tensor(
+            nc.vector.tensor_copy(
                 out=gathered[g, h][:, j, :],
-                in0=x_rows[s][:].indirect(offsets[:, h * cols : (h + 1) * cols]),
-                in1=gate_rows[h][:],
-                op=MULT,
+                in_=x_rows[s][:].indirect(offsets[:, h * cols : (h + 1) * cols]),
             )
 
         def make_x(g, h):
             x_bf = w1_bf_pool.tile([P, HALF * PACK], BF16, name="w1_bf", align_bytes=64)
-            interleave([g, h] in XV, x_bf[:], gathered[g, h][:])
+            nc.vector.tensor_tensor(
+                out=x_bf[:].rearrange("p (c i j) -> p c j i", i=PACK, j=PACK),
+                in0=gathered[g, h][:].rearrange("p j (c i) -> p c j i", i=PACK),
+                in1=gate_rows[h][:].rearrange("p (c i) -> p c i", i=PACK).unsqueeze(2).to_broadcast([P, HALF // PACK, PACK, PACK]),
+                op=MULT,
+            )
             x_mx[g, h] = quantize(keep, "x%d%d" % (g, h), x_bf[:], HALF)
 
         def make_w1(k):

@@ -20,38 +20,58 @@ P = 128
 PACK = 4
 K_PASS = P * PACK
 PASSES = K // K_PASS
+LIST_ROWS = 16
 HALVES = 2
 HALF = E * C // HALVES
-LIST_ROWS = 16
-LOADS = "xxWxWxWxWxWxWxWWwWWwWWwWWwWWwwww"
-VSET = [11,13]
-XV = []
-V2 = [7]
-HOLD = 10
-SLOTS = 9
-LAST = E * PASSES - 1
+X_PLANES = PASSES * PACK
+W1_PIECES = E * PASSES
+LAST_PIECE = W1_PIECES - 1
+
+PIECES_PER_4_PLANES = 3
+W2_LAG = 8
+FIRST_VECTOR_PIECE = 9
+SCALAR_X_BLOCKS = ((0, 0),)
+HELD_PIECE = 10
+EARLY_EXPERTS = HELD_PIECE // PASSES
+
+LOAD_BUFFERS = 10
+ROUNDED_BUFFERS = 6
+CODE_BUFFERS = 10
+HIDDEN_BANKS = 6
+
+
+def arrival_order():
+    order = []
+    pieces = 0
+    for plane in range(X_PLANES):
+        while pieces < PIECES_PER_4_PLANES * (plane + 1) // 4:
+            order.append(("w1", pieces))
+            pieces = pieces + 1
+        order.append(("x", plane))
+    for e in range(E):
+        while pieces < min(W1_PIECES, PASSES * e + W2_LAG):
+            order.append(("w1", pieces))
+            pieces = pieces + 1
+        order.append(("w2", e))
+    return order
 
 
 def tile_moe_pre_mlp_relu_kernel(tc, xT, w1, w2, gate, offs, out):
     nc = tc.nc
     with ExitStack() as ctx:
         keep = ctx.enter_context(tc.tile_pool(name="keep", bufs=1))
-        big_pool = ctx.enter_context(tc.tile_pool(name="big", bufs=1))
-        w1_bf_pool = ctx.enter_context(tc.tile_pool(name="w1_bf", bufs=10))
-        w1_mx_pool = ctx.enter_context(tc.tile_pool(name="w1_mx", bufs=8))
-        gath_pool = ctx.enter_context(tc.tile_pool(name="gath", bufs=3))
-        h_pool = ctx.enter_context(tc.tile_pool(name="h_pool", bufs=2))
+        load_pool = ctx.enter_context(tc.tile_pool(name="loads", bufs=1))
+        rounded_pool = ctx.enter_context(tc.tile_pool(name="rounded", bufs=ROUNDED_BUFFERS))
+        code_pool = ctx.enter_context(tc.tile_pool(name="codes", bufs=CODE_BUFFERS))
+        gathered_pool = ctx.enter_context(tc.tile_pool(name="gathered", bufs=PASSES * HALVES))
+        hidden_pool = ctx.enter_context(tc.tile_pool(name="hidden", bufs=2))
         small = ctx.enter_context(tc.tile_pool(name="small", bufs=2))
-        y_pool = ctx.enter_context(tc.tile_pool(name="y_pool", bufs=3))
+        y_pool = ctx.enter_context(tc.tile_pool(name="y", bufs=3))
         psum = ctx.enter_context(tc.psum_pool(name="psum", bufs=2))
-        psum_h = ctx.enter_context(tc.psum_pool(name="psum_h", bufs=6))
+        psum_hidden = ctx.enter_context(tc.psum_pool(name="psum_hidden", bufs=HIDDEN_BANKS))
 
         offsets = keep.tile([P, E * C // LIST_ROWS], U16, name="offsets")
         nc.sync.dma_start(offsets[:], offs)
-        gate_rows = {}
-        x_rows = {}
-        w1_raw = {}
-        w2_raw = {}
 
         gate_cols = keep.tile([P, HALVES, PACK], F32, name="gate_cols")
         nc.sync.dma_start(
@@ -59,150 +79,159 @@ def tile_moe_pre_mlp_relu_kernel(tc, xT, w1, w2, gate, offs, out):
             in_=gate[0, :].rearrange("(h p q) -> p h q", h=HALVES, q=PACK),
         )
 
-        def load_gate(h):
-            gate_rows[h] = keep.tile([P, HALF], F32, name="gate_row%d" % h)
-            nc.sync.dma_start(out=gate_rows[h][:], in_=gate[0:P, h * HALF : (h + 1) * HALF])
+        x_planes = {}
+        w1_raw = {}
+        w2_raw = {}
+        ring = list(range(LOAD_BUFFERS))
+        held_buffer = []
 
-        free_slots = list(range(SLOTS))
-        held = []
+        def load_buffer(shape, hold):
+            buffer = ring.pop(0)
+            (held_buffer if hold else ring).append(buffer)
+            return load_pool.tile(shape, F32, name="buffer%d" % buffer, align_bytes=64)
 
-        def slot_tile(shape, keep_slot=False):
-            slot = free_slots.pop(0)
-            if keep_slot:
-                held.append(slot)
-            else:
-                free_slots.append(slot)
-            return big_pool.tile(shape, F32, name="slot%d" % slot, align_bytes=64)
-
-        def load_x(s):
-            g, j = divmod(s, PACK)
-            x_rows[s] = keep.tile([P, T], F32, name="x_rows%d" % s)
+        def load_x(plane):
+            g, j = divmod(plane, PACK)
+            x_planes[plane] = keep.tile([P, T], F32, name="x_plane%d" % plane)
             rows = xT[g * K_PASS : (g + 1) * K_PASS, :].rearrange("(p j) t -> p j t", j=PACK)
-            nc.sync.dma_start(out=x_rows[s][:], in_=rows[:, j, :])
+            nc.sync.dma_start(out=x_planes[plane][:], in_=rows[:, j, :])
 
-        def load_w1(k):
-            e, g = divmod(k, PASSES)
+        def load_w1(piece):
+            e, g = divmod(piece, PASSES)
             rows = w1[e, g * K_PASS : (g + 1) * K_PASS, :].rearrange("(p j) c -> p j c", j=PACK)
-            if k == LAST:
-                w1_raw[k] = []
-                for a in range(2):
-                    part = slot_tile([P, PACK, H // 2])
-                    nc.sync.dma_start(out=part[:], in_=rows[:, :, a * (H // 2) : (a + 1) * (H // 2)])
-                    w1_raw[k].append(part)
-                return
-            w1_raw[k] = slot_tile([P, PACK, H], k == HOLD)
-            nc.sync.dma_start(out=w1_raw[k][:], in_=rows)
+            parts = 2 if piece == LAST_PIECE else 1
+            width = H // parts
+            w1_raw[piece] = []
+            for part in range(parts):
+                raw = load_buffer([P, PACK, width], piece == HELD_PIECE)
+                nc.sync.dma_start(out=raw[:], in_=rows[:, :, part * width : (part + 1) * width])
+                w1_raw[piece].append(raw)
 
         def load_w2(e):
-            w2_raw[e] = slot_tile([P, PACK, N])
+            w2_raw[e] = load_buffer([P, PACK, N], False)
             nc.sync.dma_start(out=w2_raw[e][:], in_=w2[e].rearrange("(p j) n -> p j n", j=PACK))
 
-        steps = []
-        seen = {"x": 0, "W": 0, "w": 0, "g": 0}
-        for ch in LOADS:
-            steps.append((ch, seen[ch]))
-            seen[ch] = seen[ch] + 1
-        loaders = {"x": load_x, "W": load_w1, "w": load_w2, "g": load_gate}
-        for ch, k in steps:
-            loaders[ch](k)
+        order = arrival_order()
+        for kind, index in order:
+            {"x": load_x, "w1": load_w1, "w2": load_w2}[kind](index)
 
-        ident = keep.tile([P, P], F32, name="ident")
-        make_identity(nc, ident[:])
-        for h in range(HALVES):
+        identity = keep.tile([P, P], F32, name="identity")
+        make_identity(nc, identity[:])
+        gate_rows = []
+        for half in range(HALVES):
             wide = small.tile([P, PACK, P], F32, name="wide")
-            nc.scalar.copy(out=wide[:], in_=gate_cols[:, h, :].unsqueeze(2).to_broadcast([P, PACK, P]))
-            spread = psum.tile([P, PACK, P], F32, name="acc_y")
+            nc.vector.tensor_copy(out=wide[:], in_=gate_cols[:, half, :].unsqueeze(2).to_broadcast([P, PACK, P]))
+            spread = psum.tile([P, PACK, P], F32, name="bank")
             for q in range(PACK):
-                nc.tensor.transpose(spread[:, q, :], wide[:, q, :], ident[:])
-            gate_rows[h] = keep.tile([P, HALF], F32, name="gate_row%d" % h)
-            mover = nc.scalar.copy
-            mover(
-                out=gate_rows[h][:].rearrange("p (n q) -> p n q", q=PACK),
+                nc.tensor.transpose(spread[:, q, :], wide[:, q, :], identity[:])
+            row = keep.tile([P, HALF], F32, name="gate_row%d" % half)
+            copy_out = nc.vector.tensor_copy if half == 0 else nc.scalar.copy
+            copy_out(
+                out=row[:].rearrange("p (n q) -> p n q", q=PACK),
                 in_=spread[:].rearrange("p q n -> p n q"),
             )
+            gate_rows.append(row)
 
-        def copy_on(on_vector, dst, src):
+        def round_copy(on_vector, dst, src):
             if on_vector:
                 nc.vector.tensor_copy(out=dst, in_=src)
             else:
                 nc.scalar.copy(out=dst, in_=src)
 
         def interleave(on_vector, dst, src):
-            copy_on(
+            round_copy(
                 on_vector,
                 dst.rearrange("p (c i j) -> p c j i", i=PACK, j=PACK),
                 src.rearrange("p j (c i) -> p c j i", i=PACK),
             )
 
-        def quantize(pool, name, grouped, width):
+        def quantize(pool, name, rounded, width):
             codes = pool.tile([P, width], U32, name=name + "_codes", align_bytes=64)
             scales = pool.tile([P, width], U8, name=name + "_scales", align_bytes=64)
-            nc.vector.quantize_mx(out=codes[:].bitcast(FP8X4), scales=scales[:], in_=grouped)
+            nc.vector.quantize_mx(out=codes[:].bitcast(FP8X4), scales=scales[:], in_=rounded)
             return codes, scales
 
         gathered = {}
         x_mx = {}
         w1_mx = {}
         w2_mx = {}
-        h_bf = {}
-        h_early = []
 
-        def gather(s, h):
-            g, j = divmod(s, PACK)
-            if j == 0:
-                gathered[g, h] = gath_pool.tile([P, PACK, HALF], F32, name="gathered")
+        def prepare_x(plane):
+            g, j = divmod(plane, PACK)
             cols = HALF // LIST_ROWS
-            nc.vector.tensor_copy(
-                out=gathered[g, h][:, j, :],
-                in_=x_rows[s][:].indirect(offsets[:, h * cols : (h + 1) * cols]),
-            )
+            for half in range(HALVES):
+                if j == 0:
+                    gathered[g, half] = gathered_pool.tile([P, PACK, HALF], F32, name="gathered")
+                nc.vector.tensor_tensor(
+                    out=gathered[g, half][:, j, :],
+                    in0=x_planes[plane][:].indirect(offsets[:, half * cols : (half + 1) * cols]),
+                    in1=gate_rows[half][:],
+                    op=MULT,
+                )
+                if j == PACK - 1:
+                    rounded = rounded_pool.tile([P, HALF * PACK], BF16, name="rounded", align_bytes=64)
+                    interleave((g, half) not in SCALAR_X_BLOCKS, rounded[:], gathered[g, half][:])
+                    x_mx[g, half] = quantize(keep, "x%d%d" % (g, half), rounded[:], HALF)
 
-        def make_x(g, h):
-            x_bf = w1_bf_pool.tile([P, HALF * PACK], BF16, name="w1_bf", align_bytes=64)
-            nc.vector.tensor_tensor(
-                out=x_bf[:].rearrange("p (c i j) -> p c j i", i=PACK, j=PACK),
-                in0=gathered[g, h][:].rearrange("p j (c i) -> p c j i", i=PACK),
-                in1=gate_rows[h][:].rearrange("p (c i) -> p c i", i=PACK).unsqueeze(2).to_broadcast([P, HALF // PACK, PACK, PACK]),
-                op=MULT,
-            )
-            x_mx[g, h] = quantize(keep, "x%d%d" % (g, h), x_bf[:], HALF)
+        def column_groups(codes, scales, count):
+            return [(codes[:, t * P : (t + 1) * P], scales[:, t * P : (t + 1) * P]) for t in range(count)]
 
-        def make_w1(k):
-            if k == LAST:
-                halves = [keep.tile([P, H * PACK // 2], BF16, name="w1_last_bf%d" % u, align_bytes=64) for u in range(2)]
-                for a in range(2):
-                    src = w1_raw[k][a][:].rearrange("p j (m t) -> p m j t", t=PACK)
-                    for u in range(2):
-                        dst = halves[u][:].rearrange("p (t m j) -> p m j t", t=2, j=PACK)
-                        copy_on(u == 0, dst[:, a * (P // 2) : (a + 1) * (P // 2), :, :], src[:, :, :, 2 * u : 2 * u + 2])
-                pairs = [quantize(keep, "w1_last%d" % u, halves[u][:], H // 2) for u in range(2)]
-                w1_mx[k] = [
-                    (pairs[t // 2][0][:, (t % 2) * P : (t % 2 + 1) * P], pairs[t // 2][1][:, (t % 2) * P : (t % 2 + 1) * P])
-                    for t in range(PACK)
-                ]
+        def prepare_w1(piece):
+            if piece == LAST_PIECE:
+                prepare_last_w1()
                 return
-            w1_bf = w1_bf_pool.tile([P, H * PACK], BF16, name="w1_bf", align_bytes=64)
-            copy_on(
-                k in VSET,
-                w1_bf[:].rearrange("p (t m j) -> p m j t", t=PACK, j=PACK),
-                w1_raw[k][:].rearrange("p j (m t) -> p m j t", t=PACK),
+            rounded = rounded_pool.tile([P, H * PACK], BF16, name="rounded", align_bytes=64)
+            round_copy(
+                piece >= FIRST_VECTOR_PIECE and piece % 2 == 1,
+                rounded[:].rearrange("p (u v m j) -> p m u j v", u=2, v=2, j=PACK),
+                w1_raw[piece][0][:].rearrange("p j (m u v) -> p m u j v", u=2, v=2),
             )
-            codes, scales = quantize(w1_mx_pool, "w1", w1_bf[:], H)
-            w1_mx[k] = [(codes[:, t * P : (t + 1) * P], scales[:, t * P : (t + 1) * P]) for t in range(PACK)]
+            codes, scales = quantize(code_pool, "w1", rounded[:], H)
+            w1_mx[piece] = column_groups(codes, scales, PACK)
 
-        def make_w2(e):
-            w2_bf = small.tile([P, N * PACK], BF16, name="w2_bf", align_bytes=64)
-            interleave(e in V2, w2_bf[:], w2_raw[e][:])
-            w2_mx[e] = quantize(keep, "w2_%d" % e, w2_bf[:], N)
+        def prepare_last_w1():
+            pair_tiles = [
+                keep.tile([P, H * PACK // 2], BF16, name="last_rounded%d" % pair, align_bytes=64) for pair in range(2)
+            ]
+            for part in range(2):
+                src = w1_raw[LAST_PIECE][part][:].rearrange("p j (m t) -> p m j t", t=PACK)
+                for pair in range(2):
+                    dst = pair_tiles[pair][:].rearrange("p (t m j) -> p m j t", t=2, j=PACK)
+                    round_copy(
+                        pair == 0,
+                        dst[:, part * (P // 2) : (part + 1) * (P // 2), :, :],
+                        src[:, :, :, 2 * pair : 2 * pair + 2],
+                    )
+            w1_mx[LAST_PIECE] = []
+            for pair in range(2):
+                codes, scales = quantize(keep, "last%d" % pair, pair_tiles[pair][:], H // 2)
+                w1_mx[LAST_PIECE].extend(column_groups(codes, scales, 2))
 
-        def first_layer(e):
-            h, place = divmod(e * C, HALF)
+        def prepare_w2(e):
+            rounded = small.tile([P, N * PACK], BF16, name="w2_rounded", align_bytes=64)
+            interleave(e == E - 1, rounded[:], w2_raw[e][:])
+            w2_mx[e] = quantize(keep, "w2_%d" % e, rounded[:], N)
+
+        hidden = {}
+        early_hidden = []
+
+        def hidden_tile(e):
+            if e >= EARLY_EXPERTS:
+                late_hidden = hidden_pool.tile([P, C * PACK], BF16, name="late_hidden", align_bytes=64)
+                return late_hidden[:]
+            if e == 0:
+                shape = [P, EARLY_EXPERTS, C * PACK]
+                early_hidden.append(load_pool.tile(shape, BF16, name="buffer%d" % held_buffer[0], align_bytes=64))
+            return early_hidden[0][:, e, :]
+
+        def first_product(e):
+            half, place = divmod(e * C, HALF)
             slots = slice(place, place + C)
-            acc = psum_h.tile([P, PACK, C], F32, name="acc_h")
+            acc = psum_hidden.tile([P, PACK, C], F32, name="acc_hidden")
             for t in range(PACK):
                 for g in range(PASSES):
                     w_codes, w_scales = w1_mx[e * PASSES + g][t]
-                    x_codes, x_scales = x_mx[g, h]
+                    x_codes, x_scales = x_mx[g, half]
                     nc.tensor.matmul_mx(
                         out=acc[:, t, :],
                         lhsT=w_codes.bitcast(FP8X4),
@@ -212,27 +241,19 @@ def tile_moe_pre_mlp_relu_kernel(tc, xT, w1, w2, gate, offs, out):
                         start=(g == 0),
                         stop=(g == PASSES - 1),
                     )
-            if 2 * e < HOLD:
-                if e == 0:
-                    h_early.append(
-                        big_pool.tile([P, (HOLD + 1) // 2, C * PACK], BF16, name="slot%d" % held[0], align_bytes=64)
-                    )
-                h_bf[e] = h_early[0][:, e, :]
-            else:
-                h_late = h_pool.tile([P, C * PACK], BF16, name="h_bf", align_bytes=64)
-                h_bf[e] = h_late[:]
+            hidden[e] = hidden_tile(e)
             nc.scalar.activation(
-                out=h_bf[e].rearrange("p (s t) -> p s t", t=PACK),
+                out=hidden[e].rearrange("p (s t) -> p s t", t=PACK),
                 in_=acc[:].rearrange("p t s -> p s t"),
                 func=RELU,
             )
 
         result = keep.tile([P, T], F32, name="result")
 
-        def second_layer(e):
-            h_codes, h_scales = quantize(small, "h", h_bf[e], C)
+        def second_product(e):
+            h_codes, h_scales = quantize(small, "h", hidden[e], C)
             w_codes, w_scales = w2_mx[e]
-            acc = psum.tile([P, C], F32, name="acc_y")
+            acc = psum.tile([P, C], F32, name="bank")
             nc.tensor.matmul_mx(
                 out=acc[:],
                 lhsT=w_codes[:].bitcast(FP8X4),
@@ -242,37 +263,22 @@ def tile_moe_pre_mlp_relu_kernel(tc, xT, w1, w2, gate, offs, out):
                 start=True,
                 stop=True,
             )
-            y_sb = y_pool.tile([P, C], F32, name="y_sb")
-            nc.scalar.copy(out=y_sb[:], in_=acc[:])
+            y = y_pool.tile([P, C], F32, name="y")
+            nc.scalar.copy(out=y[:], in_=acc[:])
             cols = C // LIST_ROWS
             nc.vector.tensor_copy(
                 out=result[:].indirect(offsets[:, e * cols : (e + 1) * cols]),
-                in_=y_sb[:],
+                in_=y[:],
             )
 
-        done = set()
-
-        def follow_ups():
-            for g in range(PASSES):
-                for h in range(HALVES):
-                    if (g, h) not in x_mx and ("x", PACK * g + PACK - 1, h) in done:
-                        make_x(g, h)
+        finished = []
+        for kind, index in order:
+            {"x": prepare_x, "w1": prepare_w1, "w2": prepare_w2}[kind](index)
             for e in range(E):
-                if e not in h_bf and (2 * e + 1) in w1_mx and (1, e * C // HALF) in x_mx and HOLD in w1_mx:
-                    first_layer(e)
-                if ("y", e) not in done and e in h_bf and e in w2_mx:
-                    second_layer(e)
-                    done.add(("y", e))
+                if e not in hidden and max(PASSES * e + PASSES - 1, HELD_PIECE) in w1_mx:
+                    first_product(e)
+                if e in hidden and e in w2_mx and e not in finished:
+                    second_product(e)
+                    finished.append(e)
 
-        for ch, k in steps:
-            if ch == "x":
-                for h in range(HALVES):
-                    gather(k, h)
-                    done.add(("x", k, h))
-                    follow_ups()
-            elif ch == "W":
-                make_w1(k)
-            elif ch == "w":
-                make_w2(k)
-            follow_ups()
         nc.sync.dma_start(out=out, in_=result[:])

@@ -28,31 +28,33 @@ W1_PIECES = E * PASSES
 LAST_PIECE = W1_PIECES - 1
 
 PIECES_PER_4_PLANES = 3
-W2_LAG = 8
+FIRST_W2_PLACE = 2
 FIRST_VECTOR_PIECE = 9
-SCALAR_X_BLOCKS = ((0, 0),)
-HELD_PIECE = 10
+HELD_PIECE = 8
 EARLY_EXPERTS = HELD_PIECE // PASSES
 
 LOAD_BUFFERS = 10
 ROUNDED_BUFFERS = 6
 CODE_BUFFERS = 10
+Y_BUFFERS = 3
 HIDDEN_BANKS = 6
+
+
+def w2_place(e):
+    return FIRST_W2_PLACE + e if e < EARLY_EXPERTS else W1_PIECES
+
+
+def x_place(plane):
+    return PIECES_PER_4_PLANES * (plane + 1) // 4
 
 
 def arrival_order():
     order = []
-    pieces = 0
-    for plane in range(X_PLANES):
-        while pieces < PIECES_PER_4_PLANES * (plane + 1) // 4:
-            order.append(("w1", pieces))
-            pieces = pieces + 1
-        order.append(("x", plane))
-    for e in range(E):
-        while pieces < min(W1_PIECES, PASSES * e + W2_LAG):
-            order.append(("w1", pieces))
-            pieces = pieces + 1
-        order.append(("w2", e))
+    for piece in range(W1_PIECES + 1):
+        order.extend(("w2", e) for e in range(E) if w2_place(e) == piece)
+        order.extend(("x", plane) for plane in range(X_PLANES) if x_place(plane) == piece)
+        if piece < W1_PIECES:
+            order.append(("w1", piece))
     return order
 
 
@@ -66,7 +68,7 @@ def tile_moe_pre_mlp_relu_kernel(tc, xT, w1, w2, gate, offs, out):
         gathered_pool = ctx.enter_context(tc.tile_pool(name="gathered", bufs=PASSES * HALVES))
         hidden_pool = ctx.enter_context(tc.tile_pool(name="hidden", bufs=2))
         small = ctx.enter_context(tc.tile_pool(name="small", bufs=2))
-        y_pool = ctx.enter_context(tc.tile_pool(name="y", bufs=3))
+        y_pool = ctx.enter_context(tc.tile_pool(name="y", bufs=Y_BUFFERS))
         psum = ctx.enter_context(tc.psum_pool(name="psum", bufs=2))
         psum_hidden = ctx.enter_context(tc.psum_pool(name="psum_hidden", bufs=HIDDEN_BANKS))
 
@@ -170,7 +172,7 @@ def tile_moe_pre_mlp_relu_kernel(tc, xT, w1, w2, gate, offs, out):
                 )
                 if j == PACK - 1:
                     rounded = rounded_pool.tile([P, HALF * PACK], BF16, name="rounded", align_bytes=64)
-                    interleave((g, half) not in SCALAR_X_BLOCKS, rounded[:], gathered[g, half][:])
+                    interleave(g == PASSES - 1, rounded[:], gathered[g, half][:])
                     x_mx[g, half] = quantize(keep, "x%d%d" % (g, half), rounded[:], HALF)
 
         def column_groups(codes, scales, count):

from contextlib import ExitStack

import concourse.mybir as mybir
from concourse.masks import make_identity

K, T, E, C, H, N = 1024, 1024, 8, 128, 512, 128
FLOPS = 2 * E * C * (K * H + H * N)
BYTES = 4 * (K * T + E * K * H + E * H * N + E * C + N * T) + 2 * 128 * (E * C // 16)

F32 = mybir.dt.float32
BF16 = mybir.dt.bfloat16
U32 = mybir.dt.uint32
U16 = mybir.dt.uint16
U8 = mybir.dt.uint8
FP8X4 = mybir.dt.float8_e4m3fn_x4
MULT = mybir.AluOpType.mult
RELU = mybir.ActivationFunctionType.Relu

P = 128
PACK = 4
K_PASS = P * PACK
PASSES = K // K_PASS
LIST_ROWS = 16
HALVES = 2
HALF = E * C // HALVES
X_PLANES = PASSES * PACK
W1_PIECES = E * PASSES
LAST_PIECE = W1_PIECES - 1

PIECES_PER_4_PLANES = 3
FIRST_W2_PLACE = 2
FIRST_VECTOR_PIECE = 9
HELD_PIECE = 8
EARLY_EXPERTS = HELD_PIECE // PASSES

LOAD_BUFFERS = 10
ROUNDED_BUFFERS = 6
CODE_BUFFERS = 10
Y_BUFFERS = 3
HIDDEN_BANKS = 6


def w2_place(e):
    return FIRST_W2_PLACE + e if e < EARLY_EXPERTS else W1_PIECES


def x_place(plane):
    return PIECES_PER_4_PLANES * (plane + 1) // 4


def arrival_order():
    order = []
    for piece in range(W1_PIECES + 1):
        order.extend(("w2", e) for e in range(E) if w2_place(e) == piece)
        order.extend(("x", plane) for plane in range(X_PLANES) if x_place(plane) == piece)
        if piece < W1_PIECES:
            order.append(("w1", piece))
    return order


def tile_moe_pre_mlp_relu_kernel(tc, xT, w1, w2, gate, offs, out):
    nc = tc.nc
    with ExitStack() as ctx:
        keep = ctx.enter_context(tc.tile_pool(name="keep", bufs=1))
        load_pool = ctx.enter_context(tc.tile_pool(name="loads", bufs=1))
        rounded_pool = ctx.enter_context(tc.tile_pool(name="rounded", bufs=ROUNDED_BUFFERS))
        code_pool = ctx.enter_context(tc.tile_pool(name="codes", bufs=CODE_BUFFERS))
        gathered_pool = ctx.enter_context(tc.tile_pool(name="gathered", bufs=PASSES * HALVES))
        hidden_pool = ctx.enter_context(tc.tile_pool(name="hidden", bufs=2))
        small = ctx.enter_context(tc.tile_pool(name="small", bufs=2))
        y_pool = ctx.enter_context(tc.tile_pool(name="y", bufs=Y_BUFFERS))
        psum = ctx.enter_context(tc.psum_pool(name="psum", bufs=2))
        psum_hidden = ctx.enter_context(tc.psum_pool(name="psum_hidden", bufs=HIDDEN_BANKS))

        offsets = keep.tile([P, E * C // LIST_ROWS], U16, name="offsets")
        nc.sync.dma_start(offsets[:], offs)

        gate_cols = keep.tile([P, HALVES, PACK], F32, name="gate_cols")
        nc.sync.dma_start(
            out=gate_cols[:],
            in_=gate[0, :].rearrange("(h p q) -> p h q", h=HALVES, q=PACK),
        )

        x_planes = {}
        w1_raw = {}
        w2_raw = {}
        ring = list(range(LOAD_BUFFERS))
        held_buffer = []

        def load_buffer(shape, hold):
            buffer = ring.pop(0)
            (held_buffer if hold else ring).append(buffer)
            return load_pool.tile(shape, F32, name="buffer%d" % buffer, align_bytes=64)

        def load_x(plane):
            g, j = divmod(plane, PACK)
            x_planes[plane] = keep.tile([P, T], F32, name="x_plane%d" % plane)
            rows = xT[g * K_PASS : (g + 1) * K_PASS, :].rearrange("(p j) t -> p j t", j=PACK)
            nc.sync.dma_start(out=x_planes[plane][:], in_=rows[:, j, :])

        def load_w1(piece):
            e, g = divmod(piece, PASSES)
            rows = w1[e, g * K_PASS : (g + 1) * K_PASS, :].rearrange("(p j) c -> p j c", j=PACK)
            parts = 2 if piece == LAST_PIECE else 1
            width = H // parts
            w1_raw[piece] = []
            for part in range(parts):
                raw = load_buffer([P, PACK, width], piece == HELD_PIECE)
                nc.sync.dma_start(out=raw[:], in_=rows[:, :, part * width : (part + 1) * width])
                w1_raw[piece].append(raw)

        def load_w2(e):
            w2_raw[e] = load_buffer([P, PACK, N], False)
            nc.sync.dma_start(out=w2_raw[e][:], in_=w2[e].rearrange("(p j) n -> p j n", j=PACK))

        order = arrival_order()
        for kind, index in order:
            {"x": load_x, "w1": load_w1, "w2": load_w2}[kind](index)

        identity = keep.tile([P, P], F32, name="identity")
        make_identity(nc, identity[:])
        gate_rows = []
        for half in range(HALVES):
            wide = small.tile([P, PACK, P], F32, name="wide")
            nc.vector.tensor_copy(out=wide[:], in_=gate_cols[:, half, :].unsqueeze(2).to_broadcast([P, PACK, P]))
            spread = psum.tile([P, PACK, P], F32, name="bank")
            for q in range(PACK):
                nc.tensor.transpose(spread[:, q, :], wide[:, q, :], identity[:])
            row = keep.tile([P, HALF], F32, name="gate_row%d" % half)
            copy_out = nc.vector.tensor_copy if half == 0 else nc.scalar.copy
            copy_out(
                out=row[:].rearrange("p (n q) -> p n q", q=PACK),
                in_=spread[:].rearrange("p q n -> p n q"),
            )
            gate_rows.append(row)

        def round_copy(on_vector, dst, src):
            if on_vector:
                nc.vector.tensor_copy(out=dst, in_=src)
            else:
                nc.scalar.copy(out=dst, in_=src)

        def interleave(on_vector, dst, src):
            round_copy(
                on_vector,
                dst.rearrange("p (c i j) -> p c j i", i=PACK, j=PACK),
                src.rearrange("p j (c i) -> p c j i", i=PACK),
            )

        def quantize(pool, name, rounded, width):
            codes = pool.tile([P, width], U32, name=name + "_codes", align_bytes=64)
            scales = pool.tile([P, width], U8, name=name + "_scales", align_bytes=64)
            nc.vector.quantize_mx(out=codes[:].bitcast(FP8X4), scales=scales[:], in_=rounded)
            return codes, scales

        gathered = {}
        x_mx = {}
        w1_mx = {}
        w2_mx = {}

        def prepare_x(plane):
            g, j = divmod(plane, PACK)
            cols = HALF // LIST_ROWS
            for half in range(HALVES):
                if j == 0:
                    gathered[g, half] = gathered_pool.tile([P, PACK, HALF], F32, name="gathered")
                nc.vector.tensor_tensor(
                    out=gathered[g, half][:, j, :],
                    in0=x_planes[plane][:].indirect(offsets[:, half * cols : (half + 1) * cols]),
                    in1=gate_rows[half][:],
                    op=MULT,
                )
                if j == PACK - 1:
                    rounded = rounded_pool.tile([P, HALF * PACK], BF16, name="rounded", align_bytes=64)
                    interleave(g == PASSES - 1, rounded[:], gathered[g, half][:])
                    x_mx[g, half] = quantize(keep, "x%d%d" % (g, half), rounded[:], HALF)

        def column_groups(codes, scales, count):
            return [(codes[:, t * P : (t + 1) * P], scales[:, t * P : (t + 1) * P]) for t in range(count)]

        def prepare_w1(piece):
            if piece == LAST_PIECE:
                prepare_last_w1()
                return
            rounded = rounded_pool.tile([P, H * PACK], BF16, name="rounded", align_bytes=64)
            round_copy(
                piece >= FIRST_VECTOR_PIECE and piece % 2 == 1,
                rounded[:].rearrange("p (u v m j) -> p m u j v", u=2, v=2, j=PACK),
                w1_raw[piece][0][:].rearrange("p j (m u v) -> p m u j v", u=2, v=2),
            )
            codes, scales = quantize(code_pool, "w1", rounded[:], H)
            w1_mx[piece] = column_groups(codes, scales, PACK)

        def prepare_last_w1():
            pair_tiles = [
                keep.tile([P, H * PACK // 2], BF16, name="last_rounded%d" % pair, align_bytes=64) for pair in range(2)
            ]
            for part in range(2):
                src = w1_raw[LAST_PIECE][part][:].rearrange("p j (m t) -> p m j t", t=PACK)
                for pair in range(2):
                    dst = pair_tiles[pair][:].rearrange("p (t m j) -> p m j t", t=2, j=PACK)
                    round_copy(
                        pair == 0,
                        dst[:, part * (P // 2) : (part + 1) * (P // 2), :, :],
                        src[:, :, :, 2 * pair : 2 * pair + 2],
                    )
            w1_mx[LAST_PIECE] = []
            for pair in range(2):
                codes, scales = quantize(keep, "last%d" % pair, pair_tiles[pair][:], H // 2)
                w1_mx[LAST_PIECE].extend(column_groups(codes, scales, 2))

        def prepare_w2(e):
            rounded = small.tile([P, N * PACK], BF16, name="w2_rounded", align_bytes=64)
            interleave(e == E - 1, rounded[:], w2_raw[e][:])
            w2_mx[e] = quantize(keep, "w2_%d" % e, rounded[:], N)

        hidden = {}
        early_hidden = []

        def hidden_tile(e):
            if e >= EARLY_EXPERTS:
                late_hidden = hidden_pool.tile([P, C * PACK], BF16, name="late_hidden", align_bytes=64)
                return late_hidden[:]
            if e == 0:
                shape = [P, EARLY_EXPERTS, C * PACK]
                early_hidden.append(load_pool.tile(shape, BF16, name="buffer%d" % held_buffer[0], align_bytes=64))
            return early_hidden[0][:, e, :]

        def first_product(e):
            half, place = divmod(e * C, HALF)
            slots = slice(place, place + C)
            acc = psum_hidden.tile([P, PACK, C], F32, name="acc_hidden")
            for t in range(PACK):
                for g in range(PASSES):
                    w_codes, w_scales = w1_mx[e * PASSES + g][t]
                    x_codes, x_scales = x_mx[g, half]
                    nc.tensor.matmul_mx(
                        out=acc[:, t, :],
                        lhsT=w_codes.bitcast(FP8X4),
                        lhsT_scale=w_scales,
                        rhs=x_codes[:, slots].bitcast(FP8X4),
                        rhs_scale=x_scales[:, slots],
                        start=(g == 0),
                        stop=(g == PASSES - 1),
                    )
            hidden[e] = hidden_tile(e)
            nc.scalar.activation(
                out=hidden[e].rearrange("p (s t) -> p s t", t=PACK),
                in_=acc[:].rearrange("p t s -> p s t"),
                func=RELU,
            )

        result = keep.tile([P, T], F32, name="result")

        def second_product(e):
            h_codes, h_scales = quantize(small, "h", hidden[e], C)
            w_codes, w_scales = w2_mx[e]
            acc = psum.tile([P, C], F32, name="bank")
            nc.tensor.matmul_mx(
                out=acc[:],
                lhsT=w_codes[:].bitcast(FP8X4),
                lhsT_scale=w_scales[:],
                rhs=h_codes[:].bitcast(FP8X4),
                rhs_scale=h_scales[:],
                start=True,
                stop=True,
            )
            y = y_pool.tile([P, C], F32, name="y")
            nc.scalar.copy(out=y[:], in_=acc[:])
            cols = C // LIST_ROWS
            nc.vector.tensor_copy(
                out=result[:].indirect(offsets[:, e * cols : (e + 1) * cols]),
                in_=y[:],
            )

        finished = []
        for kind, index in order:
            {"x": prepare_x, "w1": prepare_w1, "w2": prepare_w2}[kind](index)
            for e in range(E):
                if e not in hidden and max(PASSES * e + PASSES - 1, HELD_PIECE) in w1_mx:
                    first_product(e)
                if e in hidden and e in w2_mx and e not in finished:
                    second_product(e)
                    finished.append(e)

        nc.sync.dma_start(out=out, in_=result[:])
